import numpy as np
import ml_dtypes


def mxq(x, axis, fmt="e4m3"):
    dtype, down = {"e4m3": (ml_dtypes.float8_e4m3fn, 7), "e5m2": (ml_dtypes.float8_e5m2, 14)}[fmt]
    v = np.moveaxis(np.asarray(x, np.float32).astype(ml_dtypes.bfloat16).astype(np.float64), axis, -1)
    blocks = v.reshape(v.shape[:-1] + (-1, 32))
    amax = np.abs(blocks).max(-1, keepdims=True)
    byte = np.maximum(np.where(amax > 0, np.frexp(amax)[1] - 1 + 127, 0) - down, 1)
    scale = np.exp2(byte - 127.0)
    codes = (blocks / scale).astype(np.float32).astype(dtype).astype(np.float64)
    return np.moveaxis((codes * scale).reshape(v.shape), -1, axis)


WIDE = False


def mx_kscale(k):
    if not WIDE:
        return np.ones(k)
    levels = np.array([10, -10, 5, -5, 0])
    if k % 512:
        return np.exp2(np.random.permutation(np.resize(levels, k // 32))).repeat(32)
    a = np.empty((k // 512, 16))
    for p in range(k // 512):
        a[p, :8] = np.random.permutation(np.resize(levels, 8))
        for g in range(8):
            far = levels[np.abs(levels - a[p, g]) >= 10]
            a[p, g + 8] = far[np.random.randint(len(far))]
    return np.exp2(a.ravel()).repeat(32)


def f64(x):
    return np.asarray(x).astype(np.float64)


def striped(idx):
    return np.tile(np.asarray(idx).reshape(-1, 16).T, (8, 1)).astype(np.uint16)


def unstriped(offs):
    return offs[:16].T.reshape(-1).astype(np.int64)


E2M1 = np.array([0.0, 0.5, 1.0, 1.5, 2.0, 3.0, 4.0, 6.0, -0.0, -0.5, -1.0, -1.5, -2.0, -3.0, -4.0, -6.0])


def pack_weight(w, fmt):
    k, n = w.shape
    w = f64(np.asarray(w, np.float32).astype(ml_dtypes.bfloat16)).reshape(k // 32, 32, n)
    amax = np.abs(w).max(1)
    if fmt == "e4m3":
        byte = np.frexp(amax)[1] - 1 + 127 - 7
    else:
        mant, ex = np.frexp(amax / 6.0)
        byte = np.where(mant > 0.5, ex, ex - 1) + 127
    byte = np.clip(np.where(amax > 0, byte, 1), 1, 254)
    scaled = (w * np.exp2(127.0 - byte)[:, None, :]).reshape(k, n).astype(np.float32)
    by_word = np.ascontiguousarray(scaled.reshape(k // 512, 128, 4, n).transpose(0, 1, 3, 2))
    if fmt == "e4m3":
        words = by_word.astype(ml_dtypes.float8_e4m3fn).view(np.uint8)
    else:
        c = by_word.astype(ml_dtypes.float4_e2m1fn).view(np.uint8) & 0xF
        words = (c[..., 0::2] | (c[..., 1::2] << 4)).reshape(k // 512, 128, 2 * n)
    return np.ascontiguousarray(words), np.ascontiguousarray(byte.astype(np.uint8).reshape(k // 512, 16, n))


def unpack_weight(words, scales, fmt):
    g, _, n = scales.shape
    words = np.ascontiguousarray(words).reshape(g, 128, n, -1)
    if fmt == "e4m3":
        vals = words.view(ml_dtypes.float8_e4m3fn).astype(np.float64)
    else:
        nib = np.empty((g, 128, n, 4), np.uint8)
        nib[..., 0::2] = words & 0xF
        nib[..., 1::2] = words >> 4
        vals = E2M1[nib]
    vals = vals * np.repeat(np.exp2(scales.astype(np.float64) - 127.0), 8, axis=1)[..., None]
    return vals.transpose(0, 1, 3, 2).reshape(g * 512, n)


D, T, U, I, J, G = 512, 1024, 1024, 256, 512, 64


def setup_inputs():
    n = np.random.standard_normal
    idx = np.random.permutation(T)[:I]
    idx2 = np.random.permutation(U)[:J]
    fd = mx_kscale(D)
    tabbp = pack_weight(n((D, U)) / fd[:, None], "e4m3")
    return {
        "taba": (n((D, T)) * 1 / np.sqrt(D) * fd[:, None]).astype(np.float32),
        "tabb_words": tabbp[0],
        "tabb_scales": tabbp[1],
        "targ": (n((I, J)) * 1.0).astype(np.float32),
        "old": (0.3 * n((I, J))).astype(np.float32),
        "offs": striped(idx),
        "offs2": striped(idx2),
    }


def reference(taba, tabb_words, tabb_scales, targ, old, offs, offs2):
    idx = unstriped(offs)
    idx2 = unstriped(offs2)
    tabbu = unpack_weight(tabb_words, tabb_scales, "e4m3")
    tabaidxq = mxq(f64(taba)[:, idx], 0, "e4m3")
    tabbidx2g = tabbu[:, idx2]
    s = tabaidxq.T @ tabbidx2g
    p = np.exp(s)
    s1g = p.reshape(I, G, J // G).sum(axis=2)
    r1g = np.sqrt(s1g)
    z = np.sum(r1g, axis=1, keepdims=True)
    k1 = r1g / s1g / z
    kr = np.repeat(k1, J // G, axis=1)
    dkr = f64(targ) / (p * kr * 512.0 + 1.0) * 512.0 * p
    dk1 = dkr.reshape(I, G, J // G).sum(axis=2)
    dz = np.sum(dk1 * r1g / s1g / np.square(z) * (-1.0), axis=1, keepdims=True)
    dr1g = dk1 / z / s1g + dz
    ds1g = dr1g * 0.5 / np.sqrt(s1g) - dk1 / z * r1g / np.square(s1g)
    r1 = np.repeat(ds1g, J // G, axis=1)
    dp = f64(targ) / (p * kr * 512.0 + 1.0) * 512.0 * kr + r1
    ds = dp * p
    y = ds + f64(old)
    return y

@@ -1,0 +1,194 @@
+from contextlib import ExitStack
+
+import concourse.mybir as mybir
+
+D, T, U, I, J, G = 512, 1024, 1024, 256, 512, 64
+FLOPS = 2 * D * I * J
+
+F32 = mybir.dt.float32
+BF16 = mybir.dt.bfloat16
+I32 = mybir.dt.int32
+U32 = mybir.dt.uint32
+U16 = mybir.dt.uint16
+U8 = mybir.dt.uint8
+FP8X4 = mybir.dt.float8_e4m3fn_x4
+ALU = mybir.AluOpType
+ACT = mybir.ActivationFunctionType
+AX = mybir.AxisListType
+
+P = 128
+PACK = 4
+ROW_TILES = I // P
+GROUP = J // G
+QUARTER = 128
+GAIN = 512.0
+
+
+def tile_attend_bblockshares_kernel(tc, taba, tabb_words, tabb_scales, targ, old, offs, offs2, out):
+    nc = tc.nc
+    with ExitStack() as ctx:
+        sb = ctx.enter_context(tc.tile_pool(name="sb", bufs=1))
+        ps = ctx.enter_context(tc.psum_pool(name="ps", bufs=1))
+
+        list_a = sb.tile([P, I // 16], U16, name="list_a")
+        list_b = sb.tile([P, J // 16], U16, name="list_b")
+        b_words = sb.tile([P, U], I32, name="b_words")
+        b_bytes = sb.tile([P, U], U8, name="b_bytes")
+        planes = [sb.tile([P, T], F32, name="plane%d" % t) for t in range(PACK)]
+        t_rows = [sb.tile([P, J], F32, name="t_rows%d" % h) for h in range(ROW_TILES)]
+        o_rows = [sb.tile([P, J], F32, name="o_rows%d" % h) for h in range(ROW_TILES)]
+
+        nc.vector.memset(b_bytes[:].bitcast(I32), 0)
+        nc.sync.dma_start(list_b[:], offs2)
+        nc.sync.dma_start(list_a[:], offs)
+        for q in range(4):
+            nc.sync.dma_start(
+                b_bytes[32 * q : 32 * q + 4, :].bitcast(I32),
+                tabb_scales[0, 4 * q : 4 * q + 4, :].bitcast(I32),
+            )
+        taba_planes = taba.rearrange("(p t) c -> p t c", t=PACK)
+        for t in range(PACK):
+            nc.sync.dma_start(planes[t][:], taba_planes[:, t, :])
+        nc.sync.dma_start(b_words[:], tabb_words[0].rearrange("p n t -> p (n t)").bitcast(I32))
+        for h in range(ROW_TILES):
+            nc.sync.dma_start(t_rows[h][:], targ[h * P : (h + 1) * P, :])
+        for h in range(ROW_TILES):
+            nc.sync.dma_start(o_rows[h][:], old[h * P : (h + 1) * P, :])
+
+        b_scales = sb.tile([P, J], U8, name="b_scales", align_bytes=64)
+        nc.vector.tensor_copy(b_scales[:], b_bytes[:].indirect(list_b[:]))
+
+        a_bf = sb.tile([P, I, PACK], BF16, name="a_bf", align_bytes=64)
+        for t in range(PACK):
+            nc.vector.tensor_copy(a_bf[:, :, t], planes[t][:].indirect(list_a[:]))
+        a_codes = sb.tile([P, I], U32, name="a_codes", align_bytes=64)
+        a_scales = sb.tile([P, I], U8, name="a_scales", align_bytes=64)
+        nc.vector.quantize_mx(
+            out=a_codes[:].bitcast(FP8X4),
+            scales=a_scales[:],
+            in_=a_bf[:].rearrange("p i t -> p (i t)"),
+        )
+
+        b_codes = sb.tile([P, J], U32, name="b_codes", align_bytes=64)
+        p = sb.tile([P, ROW_TILES, J], F32, name="p")
+        s_sum = sb.tile([P, ROW_TILES, G], F32, name="s_sum")
+        s_inv = sb.tile([P, ROW_TILES, G], F32, name="s_inv")
+        gq = QUARTER // GROUP
+        for c in range(J // QUARTER):
+            cols = slice(c * QUARTER, (c + 1) * QUARTER)
+            nc.vector.tensor_copy(
+                b_codes[:, cols],
+                b_words[:].bitcast(U32).indirect(list_b[:, c * QUARTER // 16 : (c + 1) * QUARTER // 16]),
+            )
+        for c in range(J // QUARTER):
+            cols = slice(c * QUARTER, (c + 1) * QUARTER)
+            groups = slice(c * gq, (c + 1) * gq)
+            scores = ps.tile([P, ROW_TILES, QUARTER], F32, name="scores%d" % c)
+            for h in range(ROW_TILES):
+                rows = slice(h * P, (h + 1) * P)
+                nc.tensor.matmul_mx(
+                    out=scores[:, h, :],
+                    lhsT=a_codes[:, rows].bitcast(FP8X4),
+                    lhsT_scale=a_scales[:, rows],
+                    rhs=b_codes[:, cols].bitcast(FP8X4),
+                    rhs_scale=b_scales[:, cols],
+                    start=True,
+                    stop=True,
+                )
+            nc.scalar.activation(p[:, :, cols], scores[:], ACT.Exp)
+            nc.vector.tensor_reduce(
+                s_sum[:, :, groups],
+                p[:, :, cols].rearrange("p h (g r) -> p h g r", r=GROUP),
+                axis=AX.X,
+                op=ALU.add,
+            )
+            nc.vector.reciprocal(s_inv[:, :, groups], s_sum[:, :, groups])
+
+        y = sb.tile([P, ROW_TILES, G], F32, name="y")
+        nc.scalar.activation(y[:], s_sum[:], ACT.Abs_reciprocal_sqrt)
+        roots = sb.tile([P, ROW_TILES, G], F32, name="roots")
+        z = sb.tile([P, ROW_TILES], F32, name="z")
+        for h in range(ROW_TILES):
+            nc.scalar.activation(
+                roots[:, h, :], s_inv[:, h, :], ACT.Abs_reciprocal_sqrt, scale=GAIN * GAIN, accum_out=z[:, h : h + 1]
+            )
+        zs = sb.tile([P, ROW_TILES], F32, name="zs")
+
+        py = sb.tile([P, ROW_TILES, J], F32, name="py")
+        u = sb.tile([P, ROW_TILES, J], F32, name="u")
+        v = sb.tile([P, ROW_TILES, J], F32, name="v")
+        nw = sb.tile([P, ROW_TILES, J], F32, name="nw")
+        nw_sum = sb.tile([P, ROW_TILES, G], F32, name="nw_sum")
+        scaled = sb.tile([P, ROW_TILES, G], F32, name="scaled")
+        e = sb.tile([P, ROW_TILES, G], F32, name="e")
+        ow = sb.tile([P, ROW_TILES, J], F32, name="ow")
+        qq = sb.tile([P, ROW_TILES, J], F32, name="qq")
+        res = sb.tile([P, ROW_TILES, J], F32, name="res")
+        row_term = [sb.tile([P, 1], F32, name="row_term%d" % h) for h in range(ROW_TILES)]
+
+        def by_group(ap):
+            return ap.rearrange("p (g r) -> p g r", r=GROUP)
+
+        def spread(small, h, a, b):
+            n = (b - a) // GROUP
+            return small[:, h, a // GROUP : b // GROUP].unsqueeze(2).to_broadcast([P, n, GROUP])
+
+        def share(h, a, b):
+            nc.vector.tensor_tensor(by_group(py[:, h, a:b]), by_group(p[:, h, a:b]), spread(y, h, a, b), ALU.mult)
+
+        def inverse(h, a, b):
+            nc.scalar.activation(
+                u[:, h, a:b], py[:, h, a:b], ACT.Abs_reciprocal_sqrt, bias=1.0, scale=zs[:, h : h + 1]
+            )
+            nc.scalar.activation(v[:, h, a:b], u[:, h, a:b], ACT.Square)
+
+        def weigh(h, a, b):
+            nc.vector.scalar_tensor_tensor(
+                nw[:, h, a:b], v[:, h, a:b], 1.0, t_rows[h][:, a:b], ALU.subtract, ALU.mult
+            )
+
+        def group_sums(h):
+            nc.vector.tensor_reduce(nw_sum[:, h, :], by_group(nw[:, h, :]), axis=AX.X, op=ALU.add)
+            nc.scalar.activation(
+                scaled[:, h, :], nw_sum[:, h, :], ACT.Copy, scale=zs[:, h : h + 1], accum_out=row_term[h][:]
+            )
+
+        def add_old(h):
+            nc.vector.tensor_tensor(ow[:, h, :], o_rows[h][:], nw[:, h, :], ALU.subtract)
+
+        def group_term(h):
+            nc.vector.scalar_tensor_tensor(e[:, h, :], nw_sum[:, h, :], GAIN, y[:, h, :], ALU.mult, ALU.mult)
+
+        def back(h):
+            nc.vector.scalar_tensor_tensor(
+                by_group(qq[:, h, :]), spread(e, h, 0, J), row_term[h][:], by_group(py[:, h, :]), ALU.add, ALU.mult
+            )
+
+        def finish(h, a, b):
+            nc.vector.scalar_tensor_tensor(
+                res[:, h, a:b], qq[:, h, a:b], 0.5 / GAIN, ow[:, h, a:b], ALU.mult, ALU.add
+            )
+            nc.sync.dma_start(out[h * P : (h + 1) * P, a:b], res[:, h, a:b])
+
+        half = J // 2
+        share(0, 0, half)
+        nc.vector.reciprocal(zs[:], z[:])
+        share(0, half, J)
+        share(1, 0, J)
+        inverse(0, 0, half)
+        inverse(0, half, J)
+        inverse(1, 0, J)
+        weigh(0, 0, half)
+        weigh(0, half, J)
+        group_sums(0)
+        add_old(0)
+        weigh(1, 0, J)
+        group_term(0)
+        group_sums(1)
+        back(0)
+        add_old(1)
+        group_term(1)
+        finish(0, 0, J)
+        back(1)
+        finish(1, 0, half)
+        finish(1, half, J)

@@ -1,6 +1,7 @@
 from contextlib import ExitStack
 
 import concourse.mybir as mybir
+from concourse.masks import make_identity
 
 D, T, U, I, J, G = 512, 1024, 1024, 256, 512, 64
 FLOPS = 2 * D * I * J
@@ -39,27 +40,33 @@ def tile_attend_bblockshares_kernel(tc, taba, tabb_words, tabb_scales, targ, old
         o_rows = [sb.tile([P, J], F32, name="o_rows%d" % h) for h in range(ROW_TILES)]
 
         nc.vector.memset(b_bytes[:].bitcast(I32), 0)
-        nc.sync.dma_start(list_b[:], offs2)
+        taba_planes = taba.rearrange("(p t) c -> p t c", t=PACK)
         nc.sync.dma_start(list_a[:], offs)
+        nc.sync.dma_start(planes[0][:], taba_planes[:, 0, :])
+        nc.sync.dma_start(list_b[:], offs2)
         for q in range(4):
             nc.sync.dma_start(
                 b_bytes[32 * q : 32 * q + 4, :].bitcast(I32),
                 tabb_scales[0, 4 * q : 4 * q + 4, :].bitcast(I32),
             )
-        taba_planes = taba.rearrange("(p t) c -> p t c", t=PACK)
-        for t in range(PACK):
+        for t in range(1, PACK):
             nc.sync.dma_start(planes[t][:], taba_planes[:, t, :])
         nc.sync.dma_start(b_words[:], tabb_words[0].rearrange("p n t -> p (n t)").bitcast(I32))
         for h in range(ROW_TILES):
-            nc.sync.dma_start(t_rows[h][:], targ[h * P : (h + 1) * P, :])
-        for h in range(ROW_TILES):
             nc.sync.dma_start(o_rows[h][:], old[h * P : (h + 1) * P, :])
+        for h in range(ROW_TILES):
+            nc.sync.dma_start(t_rows[h][:], targ[h * P : (h + 1) * P, :])
+        ident = sb.tile([P, P], F32, name="ident")
+        make_identity(nc, ident[:])
 
         b_scales = sb.tile([P, J], U8, name="b_scales", align_bytes=64)
-        nc.vector.tensor_copy(b_scales[:], b_bytes[:].indirect(list_b[:]))
-
         a_bf = sb.tile([P, I, PACK], BF16, name="a_bf", align_bytes=64)
-        for t in range(PACK):
+        pair = sb.tile([P, 2, I], BF16, name="pair")
+        nc.vector.tensor_copy(pair[:, 0, :], planes[0][:].indirect(list_a[:]))
+        nc.vector.tensor_copy(b_scales[:], b_bytes[:].indirect(list_b[:]))
+        nc.vector.tensor_copy(pair[:, 1, :], planes[1][:].indirect(list_a[:]))
+        nc.scalar.copy(a_bf[:, :, 0:2], pair[:].rearrange("p t i -> p i t"))
+        for t in range(2, PACK):
             nc.vector.tensor_copy(a_bf[:, :, t], planes[t][:].indirect(list_a[:]))
         a_codes = sb.tile([P, I], U32, name="a_codes", align_bytes=64)
         a_scales = sb.tile([P, I], U8, name="a_scales", align_bytes=64)
@@ -72,7 +79,6 @@ def tile_attend_bblockshares_kernel(tc, taba, tabb_words, tabb_scales, targ, old
         b_codes = sb.tile([P, J], U32, name="b_codes", align_bytes=64)
         p = sb.tile([P, ROW_TILES, J], F32, name="p")
         s_sum = sb.tile([P, ROW_TILES, G], F32, name="s_sum")
-        s_inv = sb.tile([P, ROW_TILES, G], F32, name="s_inv")
         gq = QUARTER // GROUP
         for c in range(J // QUARTER):
             cols = slice(c * QUARTER, (c + 1) * QUARTER)
@@ -83,7 +89,7 @@ def tile_attend_bblockshares_kernel(tc, taba, tabb_words, tabb_scales, targ, old
         for c in range(J // QUARTER):
             cols = slice(c * QUARTER, (c + 1) * QUARTER)
             groups = slice(c * gq, (c + 1) * gq)
-            scores = ps.tile([P, ROW_TILES, QUARTER], F32, name="scores%d" % c)
+            scores = ps.tile([P, ROW_TILES, QUARTER], F32, name="scores%d" % c, tag="low%d" % c)
             for h in range(ROW_TILES):
                 rows = slice(h * P, (h + 1) * P)
                 nc.tensor.matmul_mx(
@@ -102,18 +108,26 @@ def tile_attend_bblockshares_kernel(tc, taba, tabb_words, tabb_scales, targ, old
                 axis=AX.X,
                 op=ALU.add,
             )
-            nc.vector.reciprocal(s_inv[:, :, groups], s_sum[:, :, groups])
+
+        half = J // 2
+        chunks = [(h, a, a + half) for h in range(ROW_TILES) for a in (0, half)]
+        n_old = sb.tile([P, ROW_TILES, J], F32, name="n_old")
+        for h in range(ROW_TILES):
+            nc.vector.tensor_scalar(n_old[:, h, :], o_rows[h][:], -1.0, None, ALU.mult)
+        turned = []
+        for c, (h, a, b) in enumerate(chunks):
+            bank = ps.tile([P, 2, P], F32, name="turned%d" % c, tag="low%d" % c)
+            turned.append(bank)
+            for n in range(2):
+                nc.tensor.matmul(
+                    bank[:, n, :], n_old[:, h, a + n * P : a + (n + 1) * P], ident[:],
+                    start=(n == 0), stop=False, is_transpose=True,
+                )
 
         y = sb.tile([P, ROW_TILES, G], F32, name="y")
-        nc.scalar.activation(y[:], s_sum[:], ACT.Abs_reciprocal_sqrt)
         roots = sb.tile([P, ROW_TILES, G], F32, name="roots")
-        z = sb.tile([P, ROW_TILES], F32, name="z")
-        for h in range(ROW_TILES):
-            nc.scalar.activation(
-                roots[:, h, :], s_inv[:, h, :], ACT.Abs_reciprocal_sqrt, scale=GAIN * GAIN, accum_out=z[:, h : h + 1]
-            )
-        zs = sb.tile([P, ROW_TILES], F32, name="zs")
-
+        z = [sb.tile([P, 1], F32, name="z%d" % h) for h in range(ROW_TILES)]
+        zs = [sb.tile([P, 1], F32, name="zs%d" % h) for h in range(ROW_TILES)]
         py = sb.tile([P, ROW_TILES, J], F32, name="py")
         u = sb.tile([P, ROW_TILES, J], F32, name="u")
         v = sb.tile([P, ROW_TILES, J], F32, name="v")
@@ -121,10 +135,11 @@ def tile_attend_bblockshares_kernel(tc, taba, tabb_words, tabb_scales, targ, old
         nw_sum = sb.tile([P, ROW_TILES, G], F32, name="nw_sum")
         scaled = sb.tile([P, ROW_TILES, G], F32, name="scaled")
         e = sb.tile([P, ROW_TILES, G], F32, name="e")
-        ow = sb.tile([P, ROW_TILES, J], F32, name="ow")
+        sums_t = sb.tile([P, len(chunks), half], F32, name="sums_t")
         qq = sb.tile([P, ROW_TILES, J], F32, name="qq")
         res = sb.tile([P, ROW_TILES, J], F32, name="res")
         row_term = [sb.tile([P, 1], F32, name="row_term%d" % h) for h in range(ROW_TILES)]
+        direct = [ps.tile([P, 2, P], F32, name="direct%d" % c) for c in range(len(chunks))]
 
         def by_group(ap):
             return ap.rearrange("p (g r) -> p g r", r=GROUP)
@@ -133,62 +148,114 @@ def tile_attend_bblockshares_kernel(tc, taba, tabb_words, tabb_scales, targ, old
             n = (b - a) // GROUP
             return small[:, h, a // GROUP : b // GROUP].unsqueeze(2).to_broadcast([P, n, GROUP])
 
-        def share(h, a, b):
+        def root_sum(h):
+            nc.vector.scalar_tensor_tensor(
+                roots[:, h, :], s_sum[:, h, :], 1.0 / GAIN, y[:, h, :], ALU.mult, ALU.mult, accum_out=z[h][:]
+            )
+
+        def share(c):
+            h, a, b = chunks[c]
             nc.vector.tensor_tensor(by_group(py[:, h, a:b]), by_group(p[:, h, a:b]), spread(y, h, a, b), ALU.mult)
 
-        def inverse(h, a, b):
-            nc.scalar.activation(
-                u[:, h, a:b], py[:, h, a:b], ACT.Abs_reciprocal_sqrt, bias=1.0, scale=zs[:, h : h + 1]
-            )
+        def inverse_root(c):
+            h, a, b = chunks[c]
+            nc.scalar.activation(u[:, h, a:b], py[:, h, a:b], ACT.Abs_reciprocal_sqrt, bias=1.0, scale=zs[h][:])
+
+        def square(c):
+            h, a, b = chunks[c]
             nc.scalar.activation(v[:, h, a:b], u[:, h, a:b], ACT.Square)
 
-        def weigh(h, a, b):
+        def weigh(c):
+            h, a, b = chunks[c]
             nc.vector.scalar_tensor_tensor(
                 nw[:, h, a:b], v[:, h, a:b], 1.0, t_rows[h][:, a:b], ALU.subtract, ALU.mult
             )
 
-        def group_sums(h):
-            nc.vector.tensor_reduce(nw_sum[:, h, :], by_group(nw[:, h, :]), axis=AX.X, op=ALU.add)
-            nc.scalar.activation(
-                scaled[:, h, :], nw_sum[:, h, :], ACT.Copy, scale=zs[:, h : h + 1], accum_out=row_term[h][:]
+        def turn(c):
+            h, a, b = chunks[c]
+            for n in range(2):
+                nc.tensor.matmul(
+                    turned[c][:, n, :], nw[:, h, a + n * P : a + (n + 1) * P], ident[:],
+                    start=False, stop=(n == 1), is_transpose=True,
+                )
+
+        def copy_out(c):
+            nc.scalar.copy(sums_t[:, c, :], turned[c][:].rearrange("p n i -> p (n i)"))
+
+        def turn_back(c):
+            for n in range(2):
+                nc.tensor.transpose(direct[c][:, n, :], sums_t[:, c, n * P : (n + 1) * P], ident[:])
+
+        def group_sums(c):
+            h, a, b = chunks[c]
+            nc.vector.tensor_reduce(
+                nw_sum[:, h, a // GROUP : b // GROUP], by_group(nw[:, h, a:b]), axis=AX.X, op=ALU.add
             )
 
-        def add_old(h):
-            nc.vector.tensor_tensor(ow[:, h, :], o_rows[h][:], nw[:, h, :], ALU.subtract)
+        def row_sum(h):
+            nc.scalar.activation(
+                scaled[:, h, :], nw_sum[:, h, :], ACT.Copy, scale=zs[h][:], accum_out=row_term[h][:]
+            )
 
         def group_term(h):
             nc.vector.scalar_tensor_tensor(e[:, h, :], nw_sum[:, h, :], GAIN, y[:, h, :], ALU.mult, ALU.mult)
 
-        def back(h):
+        def back(c):
+            h, a, b = chunks[c]
             nc.vector.scalar_tensor_tensor(
-                by_group(qq[:, h, :]), spread(e, h, 0, J), row_term[h][:], by_group(py[:, h, :]), ALU.add, ALU.mult
+                by_group(qq[:, h, a:b]), spread(e, h, a, b), row_term[h][:], by_group(py[:, h, a:b]),
+                ALU.add, ALU.mult,
             )
 
-        def finish(h, a, b):
+        def finish(c):
+            h, a, b = chunks[c]
             nc.vector.scalar_tensor_tensor(
-                res[:, h, a:b], qq[:, h, a:b], 0.5 / GAIN, ow[:, h, a:b], ALU.mult, ALU.add
+                res[:, h, a:b], qq[:, h, a:b], 0.5 / GAIN, direct[c][:].rearrange("p n i -> p (n i)"),
+                ALU.mult, ALU.subtract,
             )
             nc.sync.dma_start(out[h * P : (h + 1) * P, a:b], res[:, h, a:b])
 
-        half = J // 2
-        share(0, 0, half)
-        nc.vector.reciprocal(zs[:], z[:])
-        share(0, half, J)
-        share(1, 0, J)
-        inverse(0, 0, half)
-        inverse(0, half, J)
-        inverse(1, 0, J)
-        weigh(0, 0, half)
-        weigh(0, half, J)
+        for h in range(ROW_TILES):
+            nc.scalar.activation(y[:, h, :], s_sum[:, h, :], ACT.Abs_reciprocal_sqrt)
+        for h in range(ROW_TILES):
+            root_sum(h)
+            share(2 * h)
+            nc.vector.reciprocal(zs[h][:], z[h][:])
+            share(2 * h + 1)
+        for h in range(ROW_TILES):
+            inverse_root(2 * h)
+            inverse_root(2 * h + 1)
+            square(2 * h)
+            square(2 * h + 1)
+        weigh(0)
+        weigh(1)
+        turn(0)
+        turn(1)
         group_sums(0)
-        add_old(0)
-        weigh(1, 0, J)
-        group_term(0)
         group_sums(1)
+        row_sum(0)
+        copy_out(0)
+        copy_out(1)
+        weigh(2)
+        weigh(3)
+        turn(2)
+        turn_back(0)
+        turn(3)
+        turn_back(1)
+        group_term(0)
+        group_sums(2)
+        group_sums(3)
+        copy_out(2)
+        row_sum(1)
+        copy_out(3)
+        turn_back(2)
+        turn_back(3)
         back(0)
-        add_old(1)
-        group_term(1)
-        finish(0, 0, J)
         back(1)
-        finish(1, 0, half)
-        finish(1, half, J)
+        group_term(1)
+        finish(0)
+        finish(1)
+        back(2)
+        back(3)
+        finish(2)
+        finish(3)

@@ -60,21 +60,28 @@ def tile_attend_bblockshares_kernel(tc, taba, tabb_words, tabb_scales, targ, old
         make_identity(nc, ident[:])
 
         b_scales = sb.tile([P, J], U8, name="b_scales", align_bytes=64)
-        a_bf = sb.tile([P, I, PACK], BF16, name="a_bf", align_bytes=64)
-        pair = sb.tile([P, 2, I], BF16, name="pair")
-        nc.vector.tensor_copy(pair[:, 0, :], planes[0][:].indirect(list_a[:]))
+        picked = sb.tile([P, PACK, I], BF16, name="picked")
+        nc.vector.tensor_copy(picked[:, 0, :], planes[0][:].indirect(list_a[:]))
         nc.vector.tensor_copy(b_scales[:], b_bytes[:].indirect(list_b[:]))
-        nc.vector.tensor_copy(pair[:, 1, :], planes[1][:].indirect(list_a[:]))
-        nc.scalar.copy(a_bf[:, :, 0:2], pair[:].rearrange("p t i -> p i t"))
-        for t in range(2, PACK):
-            nc.vector.tensor_copy(a_bf[:, :, t], planes[t][:].indirect(list_a[:]))
+        for t in range(1, PACK - 1):
+            nc.vector.tensor_copy(picked[:, t, :], planes[t][:].indirect(list_a[:]))
+        a_bf = sb.tile([P, I, PACK], BF16, name="a_bf", align_bytes=64)
         a_codes = sb.tile([P, I], U32, name="a_codes", align_bytes=64)
         a_scales = sb.tile([P, I], U8, name="a_scales", align_bytes=64)
-        nc.vector.quantize_mx(
-            out=a_codes[:].bitcast(FP8X4),
-            scales=a_scales[:],
-            in_=a_bf[:].rearrange("p i t -> p (i t)"),
-        )
+        row_tiles = [slice(h * P, (h + 1) * P) for h in range(ROW_TILES)]
+        for h, rows in enumerate(row_tiles):
+            nc.vector.tensor_copy(
+                picked[:, PACK - 1, rows],
+                planes[PACK - 1][:].indirect(list_a[:, h * P // 16 : (h + 1) * P // 16]),
+            )
+        for rows in row_tiles:
+            nc.vector.tensor_copy(a_bf[:, rows, :], picked[:, :, rows].rearrange("p t i -> p i t"))
+        for rows in row_tiles:
+            nc.vector.quantize_mx(
+                out=a_codes[:, rows].bitcast(FP8X4),
+                scales=a_scales[:, rows],
+                in_=a_bf[:, rows, :].rearrange("p i t -> p (i t)"),
+            )
 
         b_codes = sb.tile([P, J], U32, name="b_codes", align_bytes=64)
         p = sb.tile([P, ROW_TILES, J], F32, name="p")

from contextlib import ExitStack

import concourse.mybir as mybir
from concourse.masks import make_identity

D, T, U, I, J, G = 512, 1024, 1024, 256, 512, 64
FLOPS = 2 * D * I * J

F32 = mybir.dt.float32
BF16 = mybir.dt.bfloat16
I32 = mybir.dt.int32
U32 = mybir.dt.uint32
U16 = mybir.dt.uint16
U8 = mybir.dt.uint8
FP8X4 = mybir.dt.float8_e4m3fn_x4
ALU = mybir.AluOpType
ACT = mybir.ActivationFunctionType
AX = mybir.AxisListType

P = 128
PACK = 4
ROW_TILES = I // P
GROUP = J // G
QUARTER = 128
GAIN = 512.0


def tile_attend_bblockshares_kernel(tc, taba, tabb_words, tabb_scales, targ, old, offs, offs2, out):
    nc = tc.nc
    with ExitStack() as ctx:
        sb = ctx.enter_context(tc.tile_pool(name="sb", bufs=1))
        ps = ctx.enter_context(tc.psum_pool(name="ps", bufs=1))

        list_a = sb.tile([P, I // 16], U16, name="list_a")
        list_b = sb.tile([P, J // 16], U16, name="list_b")
        b_words = sb.tile([P, U], I32, name="b_words")
        b_bytes = sb.tile([P, U], U8, name="b_bytes")
        planes = [sb.tile([P, T], F32, name="plane%d" % t) for t in range(PACK)]
        t_rows = [sb.tile([P, J], F32, name="t_rows%d" % h) for h in range(ROW_TILES)]
        o_rows = [sb.tile([P, J], F32, name="o_rows%d" % h) for h in range(ROW_TILES)]

        nc.vector.memset(b_bytes[:].bitcast(I32), 0)
        taba_planes = taba.rearrange("(p t) c -> p t c", t=PACK)
        nc.sync.dma_start(list_a[:], offs)
        nc.sync.dma_start(planes[0][:], taba_planes[:, 0, :])
        nc.sync.dma_start(list_b[:], offs2)
        for q in range(4):
            nc.sync.dma_start(
                b_bytes[32 * q : 32 * q + 4, :].bitcast(I32),
                tabb_scales[0, 4 * q : 4 * q + 4, :].bitcast(I32),
            )
        for t in range(1, PACK):
            nc.sync.dma_start(planes[t][:], taba_planes[:, t, :])
        nc.sync.dma_start(b_words[:], tabb_words[0].rearrange("p n t -> p (n t)").bitcast(I32))
        for h in range(ROW_TILES):
            nc.sync.dma_start(o_rows[h][:], old[h * P : (h + 1) * P, :])
        for h in range(ROW_TILES):
            nc.sync.dma_start(t_rows[h][:], targ[h * P : (h + 1) * P, :])
        ident = sb.tile([P, P], F32, name="ident")
        make_identity(nc, ident[:])

        b_scales = sb.tile([P, J], U8, name="b_scales", align_bytes=64)
        picked = sb.tile([P, PACK, I], BF16, name="picked")
        nc.vector.tensor_copy(picked[:, 0, :], planes[0][:].indirect(list_a[:]))
        nc.vector.tensor_copy(b_scales[:], b_bytes[:].indirect(list_b[:]))
        for t in range(1, PACK - 1):
            nc.vector.tensor_copy(picked[:, t, :], planes[t][:].indirect(list_a[:]))
        a_bf = sb.tile([P, I, PACK], BF16, name="a_bf", align_bytes=64)
        a_codes = sb.tile([P, I], U32, name="a_codes", align_bytes=64)
        a_scales = sb.tile([P, I], U8, name="a_scales", align_bytes=64)
        row_tiles = [slice(h * P, (h + 1) * P) for h in range(ROW_TILES)]
        for h, rows in enumerate(row_tiles):
            nc.vector.tensor_copy(
                picked[:, PACK - 1, rows],
                planes[PACK - 1][:].indirect(list_a[:, h * P // 16 : (h + 1) * P // 16]),
            )
        for rows in row_tiles:
            nc.vector.tensor_copy(a_bf[:, rows, :], picked[:, :, rows].rearrange("p t i -> p i t"))
        for rows in row_tiles:
            nc.vector.quantize_mx(
                out=a_codes[:, rows].bitcast(FP8X4),
                scales=a_scales[:, rows],
                in_=a_bf[:, rows, :].rearrange("p i t -> p (i t)"),
            )

        b_codes = sb.tile([P, J], U32, name="b_codes", align_bytes=64)
        p = sb.tile([P, ROW_TILES, J], F32, name="p")
        s_sum = sb.tile([P, ROW_TILES, G], F32, name="s_sum")
        gq = QUARTER // GROUP
        for c in range(J // QUARTER):
            cols = slice(c * QUARTER, (c + 1) * QUARTER)
            nc.vector.tensor_copy(
                b_codes[:, cols],
                b_words[:].bitcast(U32).indirect(list_b[:, c * QUARTER // 16 : (c + 1) * QUARTER // 16]),
            )
        for c in range(J // QUARTER):
            cols = slice(c * QUARTER, (c + 1) * QUARTER)
            groups = slice(c * gq, (c + 1) * gq)
            scores = ps.tile([P, ROW_TILES, QUARTER], F32, name="scores%d" % c, tag="low%d" % c)
            for h in range(ROW_TILES):
                rows = slice(h * P, (h + 1) * P)
                nc.tensor.matmul_mx(
                    out=scores[:, h, :],
                    lhsT=a_codes[:, rows].bitcast(FP8X4),
                    lhsT_scale=a_scales[:, rows],
                    rhs=b_codes[:, cols].bitcast(FP8X4),
                    rhs_scale=b_scales[:, cols],
                    start=True,
                    stop=True,
                )
            nc.scalar.activation(p[:, :, cols], scores[:], ACT.Exp)
            nc.vector.tensor_reduce(
                s_sum[:, :, groups],
                p[:, :, cols].rearrange("p h (g r) -> p h g r", r=GROUP),
                axis=AX.X,
                op=ALU.add,
            )

        half = J // 2
        chunks = [(h, a, a + half) for h in range(ROW_TILES) for a in (0, half)]
        n_old = sb.tile([P, ROW_TILES, J], F32, name="n_old")
        for h in range(ROW_TILES):
            nc.vector.tensor_scalar(n_old[:, h, :], o_rows[h][:], -1.0, None, ALU.mult)
        turned = []
        for c, (h, a, b) in enumerate(chunks):
            bank = ps.tile([P, 2, P], F32, name="turned%d" % c, tag="low%d" % c)
            turned.append(bank)
            for n in range(2):
                nc.tensor.matmul(
                    bank[:, n, :], n_old[:, h, a + n * P : a + (n + 1) * P], ident[:],
                    start=(n == 0), stop=False, is_transpose=True,
                )

        y = sb.tile([P, ROW_TILES, G], F32, name="y")
        roots = sb.tile([P, ROW_TILES, G], F32, name="roots")
        z = [sb.tile([P, 1], F32, name="z%d" % h) for h in range(ROW_TILES)]
        zs = [sb.tile([P, 1], F32, name="zs%d" % h) for h in range(ROW_TILES)]
        py = sb.tile([P, ROW_TILES, J], F32, name="py")
        u = sb.tile([P, ROW_TILES, J], F32, name="u")
        v = sb.tile([P, ROW_TILES, J], F32, name="v")
        nw = sb.tile([P, ROW_TILES, J], F32, name="nw")
        nw_sum = sb.tile([P, ROW_TILES, G], F32, name="nw_sum")
        scaled = sb.tile([P, ROW_TILES, G], F32, name="scaled")
        e = sb.tile([P, ROW_TILES, G], F32, name="e")
        sums_t = sb.tile([P, len(chunks), half], F32, name="sums_t")
        qq = sb.tile([P, ROW_TILES, J], F32, name="qq")
        res = sb.tile([P, ROW_TILES, J], F32, name="res")
        row_term = [sb.tile([P, 1], F32, name="row_term%d" % h) for h in range(ROW_TILES)]
        direct = [ps.tile([P, 2, P], F32, name="direct%d" % c) for c in range(len(chunks))]

        def by_group(ap):
            return ap.rearrange("p (g r) -> p g r", r=GROUP)

        def spread(small, h, a, b):
            n = (b - a) // GROUP
            return small[:, h, a // GROUP : b // GROUP].unsqueeze(2).to_broadcast([P, n, GROUP])

        def root_sum(h):
            nc.vector.scalar_tensor_tensor(
                roots[:, h, :], s_sum[:, h, :], 1.0 / GAIN, y[:, h, :], ALU.mult, ALU.mult, accum_out=z[h][:]
            )

        def share(c):
            h, a, b = chunks[c]
            nc.vector.tensor_tensor(by_group(py[:, h, a:b]), by_group(p[:, h, a:b]), spread(y, h, a, b), ALU.mult)

        def inverse_root(c):
            h, a, b = chunks[c]
            nc.scalar.activation(u[:, h, a:b], py[:, h, a:b], ACT.Abs_reciprocal_sqrt, bias=1.0, scale=zs[h][:])

        def square(c):
            h, a, b = chunks[c]
            nc.scalar.activation(v[:, h, a:b], u[:, h, a:b], ACT.Square)

        def weigh(c):
            h, a, b = chunks[c]
            nc.vector.scalar_tensor_tensor(
                nw[:, h, a:b], v[:, h, a:b], 1.0, t_rows[h][:, a:b], ALU.subtract, ALU.mult
            )

        def turn(c):
            h, a, b = chunks[c]
            for n in range(2):
                nc.tensor.matmul(
                    turned[c][:, n, :], nw[:, h, a + n * P : a + (n + 1) * P], ident[:],
                    start=False, stop=(n == 1), is_transpose=True,
                )

        def copy_out(c):
            nc.scalar.copy(sums_t[:, c, :], turned[c][:].rearrange("p n i -> p (n i)"))

        def turn_back(c):
            for n in range(2):
                nc.tensor.transpose(direct[c][:, n, :], sums_t[:, c, n * P : (n + 1) * P], ident[:])

        def group_sums(c):
            h, a, b = chunks[c]
            nc.vector.tensor_reduce(
                nw_sum[:, h, a // GROUP : b // GROUP], by_group(nw[:, h, a:b]), axis=AX.X, op=ALU.add
            )

        def row_sum(h):
            nc.scalar.activation(
                scaled[:, h, :], nw_sum[:, h, :], ACT.Copy, scale=zs[h][:], accum_out=row_term[h][:]
            )

        def group_term(h):
            nc.vector.scalar_tensor_tensor(e[:, h, :], nw_sum[:, h, :], GAIN, y[:, h, :], ALU.mult, ALU.mult)

        def back(c):
            h, a, b = chunks[c]
            nc.vector.scalar_tensor_tensor(
                by_group(qq[:, h, a:b]), spread(e, h, a, b), row_term[h][:], by_group(py[:, h, a:b]),
                ALU.add, ALU.mult,
            )

        def finish(c):
            h, a, b = chunks[c]
            nc.vector.scalar_tensor_tensor(
                res[:, h, a:b], qq[:, h, a:b], 0.5 / GAIN, direct[c][:].rearrange("p n i -> p (n i)"),
                ALU.mult, ALU.subtract,
            )
            nc.sync.dma_start(out[h * P : (h + 1) * P, a:b], res[:, h, a:b])

        for h in range(ROW_TILES):
            nc.scalar.activation(y[:, h, :], s_sum[:, h, :], ACT.Abs_reciprocal_sqrt)
        for h in range(ROW_TILES):
            root_sum(h)
            share(2 * h)
            nc.vector.reciprocal(zs[h][:], z[h][:])
            share(2 * h + 1)
        for h in range(ROW_TILES):
            inverse_root(2 * h)
            inverse_root(2 * h + 1)
            square(2 * h)
            square(2 * h + 1)
        weigh(0)
        weigh(1)
        turn(0)
        turn(1)
        group_sums(0)
        group_sums(1)
        row_sum(0)
        copy_out(0)
        copy_out(1)
        weigh(2)
        weigh(3)
        turn(2)
        turn_back(0)
        turn(3)
        turn_back(1)
        group_term(0)
        group_sums(2)
        group_sums(3)
        copy_out(2)
        row_sum(1)
        copy_out(3)
        turn_back(2)
        turn_back(3)
        back(0)
        back(1)
        group_term(1)
        finish(0)
        finish(1)
        back(2)
        back(3)
        finish(2)
        finish(3)
